import numpy as np, ml_dtypes
CORES = [3,11,19,27,35,43,51,59]
N = 8
BF = ml_dtypes.bfloat16
L, XS, PS, VIS, ST, SH = 256, 8, 4, 4, 3, 4
W, PN = L * XS, L * PS
def pack(x, z, c, p, q, t, w, d):
    b = lambda a: np.ascontiguousarray(a.reshape(N, 128, -1)).astype(np.float32).astype(BF)
    i = lambda a: np.ascontiguousarray(a.reshape(N, 128, -1)).astype(np.int32)
    return {"xt": b(x), "zt": b(z), "ch": i(c), "pa": i(p), "vi": i(q), "pl": i(t), "wt": i(w), "de": i(np.repeat(d.reshape(N, 8, 1), 16, axis=2))}
def parts(rng):
    top = rng.choice(np.array([3, 15, 255, 255]), (N, 8, 1, 1))
    x = rng.integers(0, top + 1, (N, 8, 16, W)); z = rng.integers(0, 256, (N, 8, 16, L))
    c, p, q = (rng.integers(0, W, (N, 8, 16, L)) for a in range(3)); q = np.where(rng.random(q.shape) < 0.1, p, q)
    t = rng.integers(0, W, (N, 8, 16, PN)); w = rng.integers(0, 256, (N, 8, 16)); d = rng.integers(3, 8, (N, 8))
    return x, z, c, p, q, t, w, d
def plant(rng, x, z, c, p, q, a, g, s):
    h = W // 2; o = rng.permutation(W); back = 37 * np.arange(16)[:, None]
    x[a, g][:, o[:h]] = rng.integers(0, 11, (16, h)); x[a, g][:, o[h:]] = rng.integers(245, 256, (16, h)); z[a, g] = 0
    e = rng.integers(0, 2, (1, L)); own, near, far = (o[rng.integers(0, h, (16, L)) + h * v] for v in (e, e, 1 - e))
    pc = np.where(s < 0, far, near); qc = np.where(s > 0, far, near)
    c[a, g] = (own - back) & (W - 1); p[a, g] = (pc - back) & (W - 1); q[a, g] = (qc - back) & (W - 1)
def small(rng, x, c, p, q, t, w, d, a, g, n):
    b = (a - ST) % N; k = np.arange(16); m = int(rng.integers(3, 7)); d[a, g] = m; w[a, g] = 0
    x[a] = x[a][:, :, :1].copy(); o = XS * int(rng.integers(0, L)) + 1; x[a, g][:, o] = 255 - x[a, g][:, o]
    hit = (o - 37 * k) & (W - 1)
    def plain(v):
        return (XS * rng.integers(0, L, (16, v)) + rng.integers(2, XS, (16, v)) - 37 * k[:, None]) & (W - 1)
    c[a, g] = plain(L); p[a, g] = plain(L); q[a, g] = plain(L); t[a, g][:, :1] = plain(1)
    lanes = 1 + rng.permutation(L - 1)[:3 * n]
    for j in range(3 * n):
        l = int(lanes[j]); r = m + (1 if j >= 2 * n else 0); st = int(rng.integers(0, 17 - r)); on = (k >= st) & (k < st + r)
        c[a, g][on, l] = hit[on]
        if j < n: q[a, g][on, l] = hit[on]
        else:
            s = np.where(on, hit, plain(1)[:, 0])
            for v in (c, p, q): v[b, g][:, l] = s
def atends(rng, hi, shape, share):
    col = rng.integers(0, 2, shape[:-2] + (1, shape[-1])); el = rng.integers(0, 2, shape)
    v = np.where(rng.random(col.shape) < 0.5, col, el) * hi
    return np.where(rng.random(shape) < share, v, rng.integers(0, hi + 1, shape))
def setup_inputs(rng):
    return pack(*parts(rng))
def setup_inputs_spread(rng):
    x, z, c, p, q, t, w, d = parts(rng)
    x = (np.exp2(8 * rng.random((N, 8, 1, W))) * rng.random((N, 8, 16, W))).astype(np.int64)
    z = (np.exp2(8 * rng.random((N, 8, 1, L))) * rng.random((N, 8, 16, L))).astype(np.int64)
    def un(shape):
        v = np.minimum(np.exp2(11 * rng.random(shape)).astype(np.int64), W) - 1
        return np.where(rng.random(shape) < 0.5, v, W - 1 - v)
    c, p, q, t = un(c.shape), un(p.shape), un(q.shape), un(t.shape)
    w = np.minimum(np.exp2(8 * rng.random(w.shape)).astype(np.int64), 256) - 1; d = np.minimum(np.exp2(4 * rng.random(d.shape)).astype(np.int64), 16)
    return pack(x, z, c, p, q, t, w, d)
def setup_inputs_ends(rng):
    x = atends(rng, 255, (N, 8, 16, W), 1.0); z = atends(rng, 255, (N, 8, 16, L), 1.0)
    one = (rng.integers(0, 16, (N, 8, 1, W)) == np.arange(16).reshape(1, 1, 16, 1)) & (rng.random((N, 8, 1, W)) < 0.3)
    x = np.where(one, np.abs(x - 1), x)
    c, p, q = (atends(rng, W - 1, (N, 8, 16, L), 0.75) for a in range(3)); t = atends(rng, W - 1, (N, 8, 16, PN), 0.85)
    w = rng.integers(0, 2, (N, 8, 16)) * 255; w[:, 1, ::2] = 0; w[:, 2] = 255; w[:, 7] = 255
    d = np.where(rng.random((N, 8)) < 0.6, 1, 16); d[:, 0] = 1; d[:, 7] = 16; d[N - 1, 2] = 16
    k = np.arange(16); hx = (37 * k) & (W - 1); hy = (((W - 1) ** 2 >> SH) + W - 1 + 37 * k) & (W - 1)
    item = np.zeros(16, np.int64); item[0] = 255; item[1] = 2
    for a in range(N):
        for g in (2, 7):
            if (a + g + N) % 2 == 0: x[a, g][:, hx] = item[:, None]; x[a, g][:, hy] = np.where(item > 0, 0, 255)[:, None]
            else: x[a, g][:, hx] = 255; x[a, g][:, hy] = 0
            for l in (2, 5, L - 1, 3, L - 2):
                down = l in (2, 5, L - 1); z[a, g][:, l] = item; c[a, g][:, l] = 0
                p[a, g][:, l] = W - 1 if down else 0; q[a, g][:, l] = 0 if down else W - 1
    return pack(x, z, c, p, q, t, w, d)
def setup_inputs_corners(rng):
    x, z, c, p, q, t, w, d = parts(rng); k = np.arange(16)[:, None]
    tie = np.array([0, 0, -1, -1, 0, 0, 1, 1, 0, -1, -1, 0, 1, 1, 0, 1])
    for a in range(N):
        for g in range(8):
            case = (g + a) % 8
            if a == 1: case = (0, 2)[g % 2]
            if a == 2: case = (1, 3, 4)[g % 3]
            if a > 2 and a % 2 == 1 and case == 7: case = 0
            n = int(rng.integers(2, 8)); st = rng.integers(0, 17 - n, (1, L)); s = np.full((16, L), -1); d[a, g] = 16
            if case < 2: s = np.where((k >= st) & (k < st + n), -1, 1); d[a, g] = n + case
            if case == 3: s = np.full((16, L), 1); d[a, g] = 1
            if case == 4: s = np.zeros((16, L), np.int64); d[a, g] = 1
            if case == 5: s = tie[(k + rng.integers(0, 16, (1, L))) % 16]; d[a, g] = 2
            if case == 6: s = np.where(k == 15 * rng.integers(0, 2, (1, L)), -1, 1); d[a, g] = 1
            if case == 7: s[:, int(rng.integers(0, L))] = 0
            plant(rng, x, z, c, p, q, a, g, s)
            j = int(rng.integers(0, 4))
            if j == 0: w[a, g] = 0
            if j == 1: w[a, g] = 255
            if j == 2: w[a, g] = 0; w[a, g, int(rng.integers(0, 16))] = 1
    return pack(x, z, c, p, q, t, w, d)
def setup_inputs_crowd(rng):
    x, z, c, p, q, t, w, d = parts(rng); few = np.array([0, W - 1, W // 2, 3])
    for a in range(N):
        for g in range(8):
            if a in (0, 2):
                plant(rng, x, z, c, p, q, a, g, np.full((16, L), -1)); d[a, g] = int(rng.integers(3, 7))
                for v in (c, p, q): v[a, g] = v[a, g][:, :1].copy()
                if a == 2 and g == 7: l = int(rng.integers(0, L)); p[a, g][:, l] = c[a, g][:, l]; q[a, g][:, l] = c[a, g][:, l]
            elif g % 2 == 0:
                for v in (c, p, q): v[a, g] = rng.choice(few, (16, L))
                z[a, g] = z[a, g][:, rng.integers(0, 4, L)]
            else:
                t[a, g] = t[a, g][:, rng.integers(0, 3, PN)]
                if g == 3: x[a, g] = x[a, g][:, :1].copy()
                if g == 5: y = x[a, g][:, 1].copy(); x[a, g] = x[a, g][:, :1].copy(); x[a, g][:, int(rng.integers(0, W))] = y
    return pack(x, z, c, p, q, t, w, d)
def setup_inputs_close(rng):
    x, z, c, p, q, t, w, d = parts(rng); m = rng.integers(0, 256, (N, 8, 16, 1))
    x = np.where(rng.random((N, 8, 1, W)) < 0.5, m, 255 - m)
    e = (rng.integers(0, 16, (N, 8, 1, W)) == np.arange(16).reshape(1, 1, 16, 1)) * rng.integers(-1, 2, (N, 8, 1, W))
    x = np.clip(x + e, 0, 255); d = rng.integers(1, 6, (N, 8)); gs = rng.permutation(8)
    small(rng, x, c, p, q, t, w, d, 1, int(gs[0]), 1)
    small(rng, x, c, p, q, t, w, d, 3, int(gs[1]), 3)
    return pack(x, z, c, p, q, t, w, d)
def check_inputs(d):
    bad = []
    for k, lo, hi in (("xt", 0, 255), ("zt", 0, 255), ("ch", 0, W - 1), ("pa", 0, W - 1), ("vi", 0, W - 1), ("pl", 0, W - 1), ("wt", 0, 255), ("de", 1, 16)):
        v = np.asarray(d[k]).astype(np.float64)
        if not (np.min(v) >= lo and np.max(v) <= hi): bad.append("range of " + k)
        elif np.any(v != np.floor(v)): bad.append("whole numbers in " + k)
    v = np.asarray(d["de"]).reshape(N, 8, 16)
    if np.any(v != v[:, :, :1]): bad.append("de alike in a group")
    return bad
def reference(xt, zt, ch, pa, vi, pl, wt, de):
    x = xt.astype(np.float32).astype(np.int32).reshape(N, 8, 16, W); z = zt.astype(np.float32).astype(np.int64).reshape(N, 8, 16, L)
    c, p, q = (a.astype(np.int64).reshape(N, 8, 16, L) for a in (ch, pa, vi)); t = pl.astype(np.int64).reshape(N, 8, 16, PN)
    w = wt.astype(np.int64).reshape(N, 8, 16, 1); d = de.astype(np.int64).reshape(N, 8, 16)[:, :, :1]
    site = np.arange(16).reshape(1, 1, 16, 1); k = np.arange(16); lane = np.arange(L); count = np.zeros((N, 1, 1), np.int64)
    for visit in range(VIS):
        if visit > 0: q = np.roll(q, ST, axis=0)
        u = np.add.reduce(w * z, axis=2) & (W - 1)
        got = []
        for n in (c, p, q):
            h = (((n * u[:, :, None]) >> SH) + n + 37 * site) & (W - 1)
            ix = np.ascontiguousarray(h.transpose(0, 1, 3, 2)).reshape(N, 8, 1, 16 * L)
            got.append(np.take_along_axis(x, ix, 3).reshape(N, 8, 16, L, 16))
        xs, ys, vs = got
        s = np.sign(np.add.reduce(np.abs(xs - vs), axis=2) - np.add.reduce(np.abs(xs - ys), axis=2)).astype(np.int64)
        H = np.zeros((N, 8, L), np.int64); top = H; ti = H; best = H - 99; bi = H; bj = H
        for j in range(1, 17):
            H = H + s[..., j - 1]; e = top - H; win = e > best
            best = np.where(win, e, best); bi = np.where(win, ti, bi); bj = np.where(win, j, bj)
            ge = H >= top; top = np.where(ge, H, top); ti = np.where(ge, j, ti)
        run = (k >= bi[..., None]) & (k < bj[..., None])
        m = np.max(np.where(run[:, :, None], xs, 0), axis=4).astype(np.int64)
        um = np.add.reduce(w * m, axis=2) & (W - 1)
        rec = best >= d + (count & 1)
        cut = run.transpose(0, 1, 3, 2) & rec[:, :, None]
        c, q = np.where(cut, p, c), np.where(cut, c, q)
        p = np.take_along_axis(t, (um & (PN - 1))[:, :, None], 3)
        at = (PS * lane + (um & (PS - 1)))[:, :, None]
        np.put_along_axis(t, at, np.where(rec[:, :, None], c, np.take_along_axis(t, at, 3)), 3)
        ib = bi[:, :, None, :, None]
        xi = np.take_along_axis(xs, ib, 4)[..., 0]; vv = np.take_along_axis(vs, ib, 4)[..., 0]
        np.put_along_axis(x, (XS * lane + (um & (XS - 1)))[:, :, None], (xi + vv) >> 1, 3)
        z = (z + m) >> 1
        count = np.add.reduce(rec.reshape(N, 8 * L).astype(np.int64), axis=1).reshape(N, 1, 1)
    return {"yc": c.reshape(N, 128, L).astype(np.float32), "yp": p.reshape(N, 128, L).astype(np.float32), "yq": q.reshape(N, 128, L).astype(np.float32),
            "yl": t.reshape(N, 128, PN).astype(np.float32), "yx": x.reshape(N, 128, W).astype(np.float32).astype(BF), "yz": z.reshape(N, 128, L).astype(np.float32).astype(BF)}

import numpy as np
from concourse.mybir import AluOpType as ALU, AxisListType, ActivationFunctionType as ACT

NV, ST, NR = 4, 3, 8
SUPERS = [(0, 8), (8, 16)]
CHUNKS = [(0, 4), (4, 8), (8, 12), (12, 16)]
ITERS = 900
CY, PEC, GA, SC, HOP = 0.00083, 0.00072, 1.5, 3.8, 0.08

SCRATCH, SEMAPHORES = {}, ["V", "S", "P", "G", "sent", "gd"]
DTY, VIEW, TOP, WID = {}, {}, {}, {}
F, B, H, I, U = "float32", "bfloat16", "float16", "int32", "uint16"
POOLS = {F: "sf", B: "sb", H: "sh", I: "si", U: "su"}


def buf(name, shape, dtype, where="sbuf"):
    SCRATCH[name] = (where, shape, dtype)
    DTY[name] = (dtype, where)
    VIEW[name] = (name, 0)


def view(name, w, dtype):
    p = POOLS[dtype]
    VIEW[name] = (p, TOP.get(p, 0))
    DTY[name] = (dtype, "sbuf")
    TOP[p] = TOP.get(p, 0) + (w + 15) // 16 * 16
    SCRATCH[p] = ("sbuf", [128, TOP[p]], dtype)
    WID[name] = w


for _n, _w, _d in [("xtb", 2048, B), ("tab", 2688, F), ("pool", 2048, F), ("ci", 256, I), ("pi", 256, I), ("qi", 256, I), ("pli", 1024, I), ("wti", 1, I),
                   ("dei", 1, I), ("MT", 1280, B), ("z0", 256, B), ("z1", 256, B), ("cfin", 256, F), ("pfin", 256, F), ("qfin", 256, F)]:
    buf(_n, [128, _w], _d)
for _n, _w, _d in [
    ("wcol", 1, F), ("wcs", 1, F), ("decol", 1, F), ("kcol", 1, F), ("k37", 1, F), ("pint", 16, I), ("pand", 16, I), ("icol", 16, F), ("PM", 16, F),
    ("ones", 256, B), ("g1", 128, B), ("g2", 128, B), ("wf", 128, B), ("idb", 128, B), ("idm", 128, B), ("id2", 128, B),
    ("idh", 128, H), ("idhn", 128, H), ("base", 256, F), ("lane", 16, F), ("lane4", 16, F), ("l16", 16, F), ("it1", 256, F), ("it2", 256, F),
    ("mt1", 256, B), ("mt2", 256, B), ("thrc", 16, F), ("c16", 256, F), ("cnt", 1, F), ("cnti", 1, I), ("cnta", 1, I), ("cntf", 1, F), ("q0", 256, H),
]:
    view(_n, _w, _d)
for _n in ("EP", "EN", "WE", "BB"):
    buf(_n, [128, 16, 128], B)
for _v in (0, 1):
    for _n in ("X", "M", "DV", "DY", "MB"):
        buf("%s%d" % (_n, _v), [128, 4096], B)
    for _n, _w, _d in [("c", 256, H), ("p", 256, H), ("ti", 256, I), ("tu", 256, I), ("E", 264, F), ("R", 256, F), ("sg", 256, F), ("mk", 256, B), ("thr", 16, F),
                       ("rA", 256, F), ("xv", 256, B), ("x2", 256, B), ("m", 256, B), ("zA", 256, F), ("cut", 256, F), ("nrb", 16, B)]:
        view("%s%d" % (_n, _v), _w, _d)
    for _n in ("x", "y", "v"):
        view("pr%s%d" % (_n, _v), 256, I)
        view("ps%s%d" % (_n, _v), 256, I)
        view("of%s%d" % (_n, _v), 256, U)
    for _n in ("AY", "AV"):
        buf("%s%d" % (_n, _v), [128, 16, 256], B)
    for _s, (_a, _b) in enumerate(SUPERS):
        w = _b - _a
        for _n, _w, _d in [("r1", w, I), ("rn", w, I), ("rm", w, F), ("I3", 3 * w, I), ("J3", 3 * w, F), ("OF", 3 * w, U), ("um", w, I), ("U3", 3 * w, I), ("V3", 3 * w, F), ("OU", 3 * w, U)]:
            view("%s_%d%d" % (_n, _s, _v), _w, _d)
for _s, (_a, _b) in enumerate(SUPERS):
    view("ka_%d" % _s, 3 * (_b - _a), F)
    view("kb_%d" % _s, 3 * (_b - _a), F)
for _t in range(NV - 1):
    buf("QS%d" % _t, [128, 256], H)
    buf("QL%d" % _t, [128, 256], H)
    for _s in range(len(SUPERS)):
        SEMAPHORES.append("arr%d_%d" % (_t, _s))
PB, PD = ["pB0", "pB1"], ["pD0", "pD1"]
for _n in PB:
    buf(_n, [128, 8, 64], F, "psum")
for _n in PD + ["pZ", "pC", "pV", "pK"]:
    buf(_n, [128, 512], F, "psum")


def A(name, lo=0, hi=None, step=None):
    bn, off = VIEW[name]
    if hi is None:
        hi = WID[name] if name in WID else SCRATCH[name][1][1]
    n = len(range(lo, hi, step or 1))
    lo, hi = lo + off, hi + off
    return {"g": lambda T: T[bn][:, lo:hi] if step is None else T[bn][:, lo:hi:step], "r": [(bn, lo, hi)], "n": n, "name": name, "ind": False}


def A3(name, a, b, lo=0, hi=None):
    w = SCRATCH[name][1][2]
    hi = w if hi is None else hi
    return {"g": lambda T: T[name][:, a:b, lo:hi], "r": [(name, a * w, b * w)], "n": (b - a) * (hi - lo), "name": name, "ind": False}


def A3i(name, a, lo=0, hi=None, step=None):
    w = SCRATCH[name][1][2]
    hi = w if hi is None else hi
    n = len(range(lo, hi, step or 1))
    return {"g": lambda T: T[name][:, a, lo:hi] if step is None else T[name][:, a, lo:hi:step], "r": [(name, a * w, (a + 1) * w)], "n": n, "name": name, "ind": False}


def IND(win, off):
    return {"g": lambda T: win["g"](T).indirect(off["g"](T)), "r": win["r"], "off": off["r"], "n": 16 * off["n"], "name": win["name"], "ind": True}


def is2(*o):
    return all(DTY[x["name"]][0] in (B, H, U) for x in o)


def inps(o):
    return DTY[o["name"]][1] == "psum"


OPS, START = [], []


def add(q, cost, fns, reads, writes, key=None, **kw):
    R, W = [], []
    for o in reads:
        R += o["r"] + o.get("off", [])
    for o in writes:
        W += o["r"]
        R += o.get("off", [])
    d = {"q": q, "cost": cost, "fns": fns, "R": R, "W": W, "key": key}
    d.update(kw)
    ind = [o for o in reads if o["ind"]]
    d["ge"], d["se"] = (ind[0]["n"] if ind else 0), sum(o["n"] for o in writes if o["ind"])
    d["place"] = len(OPS) - START[0] if START else 0
    OPS.append(d)


def cst(q, out, n, per, ind):
    if out["ind"]:
        return 0.05 + n * SC * CY
    if ind:
        return (0.05 if q == "V" else 0.065) + n * GA * CY
    return max(64, n * per) * CY


def tt(out, a, b, op):
    per = 1 if (inps(a) or inps(b)) else 2
    add("V", cst("V", out, a["n"], per, a["ind"]), [lambda g, T: g.vector.tensor_tensor(out["g"](T), a["g"](T), b["g"](T), op)], [a, b], [out])


def ts(out, a, s1, s2, op0, op1=None):
    per = 0.5 if is2(out, a) else 1
    cols = [s for s in (s1, s2) if isinstance(s, dict)]

    def f(g, T):
        x1 = s1["g"](T) if isinstance(s1, dict) else s1
        x2 = s2["g"](T) if isinstance(s2, dict) else s2
        if op1 is None:
            return g.vector.tensor_scalar(out["g"](T), a["g"](T), x1, None, op0)
        return g.vector.tensor_scalar(out["g"](T), a["g"](T), x1, x2, op0, op1)
    add("V", cst("V", out, a["n"], per, a["ind"]), [f], [a] + cols, [out])


def vcp(out, a):
    add("V", cst("V", out, a["n"], 0.5 if is2(out, a) else 1, a["ind"]), [lambda g, T: g.vector.tensor_copy(out["g"](T), a["g"](T))], [a], [out])


def vset(out, c):
    add("V", cst("V", out, out["n"], 1, False), [lambda g, T: g.vector.memset(out["g"](T), c)], [], [out])


def scan(out, d0, d1, init, op0, op1):
    add("V", cst("V", out, out["n"], 0.5 if is2(out, d0, d1) else 1, False),
        [lambda g, T: g.vector.tensor_tensor_scan(out["g"](T), d0["g"](T), d1["g"](T), init, op0, op1)], [d0, d1], [out])


def act(out, a, func, bias=0.0, scale=1.0):
    cols = [s for s in (bias, scale) if isinstance(s, dict)]

    def f(g, T):
        return g.scalar.activation(out["g"](T), a["g"](T), func, bias=bias["g"](T) if isinstance(bias, dict) else bias,
                                   scale=scale["g"](T) if isinstance(scale, dict) else scale)
    add("S", cst("S", out, a["n"], 1, a["ind"]), [f], [a] + cols, [out])


def mms(group):
    fns = [(lambda o, l, r, s, e: lambda g, T: g.tensor.matmul(o["g"](T), l["g"](T), r["g"](T), s, e))(*x) for x in group]
    add("P", sum(max(64, x[2]["n"]) * PEC for x in group), fns, [x[1] for x in group] + [x[2] for x in group], [x[0] for x in group])


def dma_sem():
    k = "d%d" % len(SEMAPHORES)
    SEMAPHORES.append(k)
    return k


def load(out, src):
    add("Y", 0.1, [lambda g, T: g.sync.dma_start(out["g"](T), T[src][:])], [], [out], key=dma_sem(), lat=2.5)


def store(dst, a, lo=None, hi=None, cast=False):
    if cast:
        add("G", 1.2, [lambda g, T: g.dma_start(T[dst][:], a["g"](T))], [a], [], key="gd", lat=3.0)
    else:
        add("Y", 0.1, [lambda g, T: g.sync.dma_start(T[dst][:, lo:hi], a["g"](T))], [a], [], key=dma_sem(), lat=2.5)


def gi(out, pattern, base, cm):
    f = DTY[out["name"]][0] != I
    add("G", 0.13 + 2 * out["n"] * CY, [lambda g, T: g.iota(out["g"](T), pattern, base, cm, allow_small_or_imprecise_dtypes=True) if f else g.iota(out["g"](T), pattern, base, cm)], [], [out])


def gsel(out, a, pattern, op, base, cm):
    add("G", 0.17 + 2 * out["n"] * CY, [lambda g, T: g.affine_select(out["g"](T), a["g"](T), pattern, op, 0.0, base, cm)], [a], [out])


def constants():
    for tile, src in (("ci", "ch"), ("z0", "zt"), ("wti", "wt"), ("xtb", "xt"), ("pi", "pa"), ("qi", "vi"), ("dei", "de"), ("pli", "pl")):
        load(A(tile), src)
    vset(A("ones"), 1.0)
    vset(A("c16"), 16.0)
    gi(A("pint"), [[0, 16]], 0, 1)
    gsel(A("g1"), A("ones", 0, 128), [[-16, 8], [0, 16]], ALU.is_ge, 0, 1)
    gsel(A("g2"), A("g1"), [[16, 8], [0, 16]], ALU.is_ge, 15, -1)
    gi(A("icol"), [[1, 16]], 0, 0)
    gsel(A("idb"), A("ones", 0, 128), [[-1, 128]], ALU.is_equal, 0, 1)
    gi(A("base"), [[8192, 16], [1, 16]], 0, 0)
    gi(A("l16"), [[16, 16]], 0, 0)
    gi(A("it1"), [[0, 16], [1, 16]], 0, 0)
    gi(A("it2"), [[-1, 16], [0, 16]], 15, 0)
    gi(A("MT", 256, 1280), [[0, 1024]], 0, 0)
    vcp(A("pV", 256, 512), A("base"))
    ts(A("pand"), A("pint"), 15, None, ALU.bitwise_and)
    vcp(A("kcol"), A("pand", 0, 1))
    ts(A("k37"), A("kcol"), 37.0, None, ALU.mult)
    tt(A("PM"), A("pand"), A("icol"), ALU.is_equal)
    vcp(A("wcol"), A("wti"))
    ts(A("wf"), A("g2"), A("wcol"), None, ALU.mult)
    half = 1024
    act(A("tab", 0, half), A("xtb", 0, half), ACT.Copy)
    act(A("tab", half, 2048), A("xtb", half, 2048), ACT.Copy)
    act(A("tab", 2048, 2688), A("xtb", 0, 640), ACT.Copy)
    vcp(A("c0"), A("ci"))
    hash_u(0, 0, 16)
    hash_list("x", 0, "c0", 0, 16)
    vcp(A("p0"), A("pi"))
    hash_list("y", 0, "p0", 0, 16)
    vcp(A("q0"), A("qi"))
    hash_list("v", 0, "q0", 0, 16)
    add("V", 0.9, [lambda g, T: g.vector.memset(T.EP[:, :, :], 0.0)], [], [A3("EP", 0, 16)])
    for b in range(16):
        act(A3i("EP", b, b, 128, 16), A("g2", b, 128, 16), ACT.Copy, scale=256.0)
    for b in range(16):
        ts(A3i("EN", b), A3i("EP", b), -1.0, None, ALU.mult)
    for b in range(16):
        ts(A3i("BB", b), A("g2"), A("PM", b, b + 1), None, ALU.mult)
    vcp(A("decol"), A("dei"))
    ts(A("decol"), A("decol"), 256.0, None, ALU.mult)
    ts(A("thrc"), A("base", 0, 256, 16), A("decol"), None, ALU.add)
    ts(A("lane"), A("l16"), A("kcol"), None, ALU.add)
    ts(A("lane4"), A("lane"), 4.0, None, ALU.mult)
    act(A("idm"), A("idb"), ACT.Copy, scale=-0.5)
    act(A("id2"), A("idb"), ACT.Copy, scale=2.0)
    ts(A("mt1"), A("it1"), A("kcol"), None, ALU.is_le)
    ts(A("mt2"), A("it2"), A("kcol"), None, ALU.is_ge)
    tt(A("MT", 0, 256), A("mt1"), A("mt2"), ALU.mult)
    for s, (a, b) in enumerate(SUPERS):
        w = b - a
        ts(A("ka_%d" % s, w, 2 * w), A("lane", a, b), 16.0, -256.0 * a, ALU.mult, ALU.add)
        ts(A("ka_%d" % s, 2 * w, 3 * w), A("lane", a, b), 16.0, -256.0 * a, ALU.mult, ALU.add)
        ts(A("kb_%d" % s, 0, w), A("lane", a, b), 8.0, None, ALU.mult)
        vset(A("kb_%d" % s, w, 2 * w), 0.0)
    for v in (0, 1):
        vset(A("E%d" % v, 0, 8), -1000000.0)
    ts(A("wcs"), A("wcol"), 1.0 / 256, None, ALU.mult)
    for b in range(16):
        act(A3i("WE", b), A3i("EP", b), ACT.Copy, scale=A("wcs"))
    vcp(A("idh"), A("idb"))
    ts(A("idhn"), A("idb"), -1.0, None, ALU.mult)
    vcp(A("pool", 0, 1024), A("pli"))


def hash_u(t, a, b):
    v = t % 2
    lo, hi = 16 * a, 16 * b
    mms([(A("pZ", lo, hi), A("wf"), A("z%d" % v, lo, hi), True, True)])
    vcp(A("ti%d" % v, lo, hi), A("pZ", lo, hi))
    ts(A("tu%d" % v, lo, hi), A("ti%d" % v, lo, hi), 2047, None, ALU.bitwise_and)
    ts(A("pV", lo, hi), A("tu%d" % v, lo, hi), 16.0, None, ALU.add)


def hash_list(n, t, src, a, b):
    v = t % 2
    lo, hi = 16 * a, 16 * b
    pr, ps, of = ["%s%s%d" % (k, n, v) for k in ("pr", "ps", "of")]
    tt(A(pr, lo, hi), A(src, lo, hi), A("pV", lo, hi), ALU.mult)
    ts(A(ps, lo, hi), A(pr, lo, hi), 4, 2047, ALU.arith_shift_right, ALU.bitwise_and)
    ts(A(of, lo, hi), A(ps, lo, hi), A("k37"), None, ALU.add)


def chunk(t, ci):
    a, b = CHUNKS[ci]
    v, n = t % 2, 16 * (b - a)
    lo, hi = 16 * a, 16 * b
    X, M, DV, DY, AY, AV, MB, E, sg, mk = ["%s%d" % (k, v) for k in ("X", "M", "DV", "DY", "AY", "AV", "MB", "E", "sg", "mk")]
    act(A(X, 16 * lo, 16 * hi), IND(A("tab"), A("ofx%d" % v, lo, hi)), ACT.Copy)
    tt(A(DY, 16 * lo, 16 * hi), IND(A("tab"), A("ofy%d" % v, lo, hi)), A(X, 16 * lo, 16 * hi), ALU.subtract)
    act(A3(AY, a, b), A(DY, 16 * lo, 16 * hi), ACT.Abs)
    tt(A(DV, 16 * lo, 16 * hi), IND(A("tab"), A("ofv%d" % v, lo, hi)), A(X, 16 * lo, 16 * hi), ALU.subtract)
    act(A3(AV, a, b), A(DV, 16 * lo, 16 * hi), ACT.Abs)
    bank = PD[(t * len(CHUNKS) + ci) % 2]
    mms([(A(bank, 0, n), A3i("EP", k), A3(AY, a, b, 16 * k, 16 * k + 16), k == 0, False) for k in range(16)])
    mms([(A(bank, 0, n), A3i("EN", k), A3(AV, a, b, 16 * k, 16 * k + 16), False, k == 15) for k in range(16)])
    ts(A(sg, lo, hi), A(bank, 0, n), 256.0, -256.0, ALU.min, ALU.max)
    scan(A(E, 8 + lo, 8 + hi), A("base", lo, hi), A(sg, lo, hi), -1000000.0, ALU.max, ALU.add)
    tt(A(mk, lo, hi), A(E, 7 + lo, 7 + hi), A("pV", 256 + lo, 256 + hi), ALU.is_gt)
    for h in (0, 1):
        bank = PB[h]
        mms([(A3i(bank, k, 0, n), A3i("BB", 8 * h + k), A(mk, lo, hi), True, True) for k in range(8)])
        for l in range(a, b):
            act(A(MB, 256 * l + 128 * h, 256 * l + 128 * h + 128), A3(bank, 0, 8, 16 * (l - a), 16 * (l - a) + 16), ACT.Copy)
    scan(A(M, 16 * lo, 16 * hi), A(MB, 16 * lo, 16 * hi), A(X, 16 * lo, 16 * hi), 0.0, ALU.mult, ALU.max)


def small(t, s):
    a, b = SUPERS[s]
    v, w = t % 2, b - a
    lo, hi = 16 * a, 16 * b
    last = t == NV - 1
    nv = 1 - v

    def N(k):
        return "%s%d" % (k, v)

    def S(k):
        return "%s_%d%d" % (k, s, v)
    ka, kb, nz = "ka_%d" % s, "kb_%d" % s, "z%d" % nv
    scan(A(N("R"), lo, hi), A("c16", lo, hi), A(N("E"), 8 + lo, 8 + hi), -1000000.0, ALU.add, ALU.max)
    end = A(N("R"), lo + 15, hi, 16)
    vcp(A(S("r1")), end)
    ts(A(S("rn")), end, -1.0, -1.0, ALU.mult, ALU.add)
    tt(A(S("rm")), end, A(N("thr") if t else "thrc", a, b), ALU.subtract)
    ts(A(ka, 0, w), A(S("rm")), 0.0, 1024.0, ALU.is_lt, ALU.mult)
    ts(A(S("I3"), 0, w), A(S("r1")), 255, None, ALU.bitwise_and)
    ts(A(S("I3"), w, 2 * w), A(S("r1")), 15, None, ALU.bitwise_and)
    ts(A(S("I3"), 2 * w, 3 * w), A(S("rn")), 4, 15, ALU.arith_shift_right, ALU.bitwise_and)
    tt(A(S("J3")), A(S("I3")), A(ka), ALU.add)
    vcp(A(S("OF")), A(S("J3")))
    act(A(N("m"), lo, hi), IND(A(N("M"), 16 * lo, 16 * hi), A(S("OF"), 2 * w, 3 * w)), ACT.Copy)
    k0, k1 = 256 + lo, 256 + hi
    half = (A("idm"), A("ones", 0, hi - lo), False, True)
    mms([(A("pK", lo, hi), A("idb"), A(N("m"), lo, hi), True, False), (A("pK", lo, hi), A("idb"), A(N("z"), lo, hi), False, False), (A("pK", lo, hi),) + half])
    xo = A(S("OF"), w, 2 * w)
    act(A(N("x2"), lo, hi), IND(A(N("X"), 16 * lo, 16 * hi), xo), ACT.Copy)
    act(A(N("xv"), lo, hi), IND(A(N("DV"), 16 * lo, 16 * hi), xo), ACT.Copy)
    mms([(A("pK", k0, k1), A("id2"), A(N("x2"), lo, hi), True, False), (A("pK", k0, k1), A("idb"), A(N("xv"), lo, hi), False, False), (A("pK", k0, k1),) + half])
    act(A(N("rA"), lo, hi), A("pK", k0, k1), ACT.Identity, bias=16777216.0)
    mms([(A("pZ", 256 + 32 * s, 256 + 32 * s + w), A3i("WE", k), A(N("m"), lo + k, hi, 16), k == 0, k == 15) for k in range(16)])
    vcp(A(S("um")), A("pZ", 256 + 32 * s, 256 + 32 * s + w))
    ts(A(S("U3"), 0, w), A(S("um")), 7, None, ALU.bitwise_and)
    ts(A(S("U3"), w, 2 * w), A(S("um")), 1023, None, ALU.bitwise_and)
    ts(A(S("U3"), 2 * w, 3 * w), A(S("um")), 3, None, ALU.bitwise_and)
    tt(A(kb, 2 * w, 3 * w), A("lane4", a, b), A(ka, 0, w), ALU.add)
    tt(A(S("V3")), A(S("U3")), A(kb), ALU.add)
    vcp(A(S("OU")), A(S("V3")))
    act(A(N("zA"), lo, hi), A("pK", lo, hi), ACT.Identity, bias=16777216.0)
    act(A(nz, lo, hi), A(N("zA"), lo, hi), ACT.Identity, bias=-8388608.0, scale=0.5)
    qn = "q0" if t == 0 else "QL%d" % (t - 1)
    cn, pn = "c%d" % v, "p%d" % v
    mms([(A("pC", 2 * lo, lo + hi), A("idh"), A(cn, lo, hi), True, False), (A("pC", 2 * lo, lo + hi), A("idhn"), A(qn, lo, hi), False, True)])
    mms([(A("pC", lo + hi, 2 * hi), A("idh"), A(pn, lo, hi), True, False), (A("pC", lo + hi, 2 * hi), A("idhn"), A(cn, lo, hi), False, True)])
    act(A(N("cut"), lo, hi), IND(A("MT"), A(S("OF"), 0, w)), ACT.Copy)
    tt(A("pC", 2 * lo, lo + hi), A("pC", 2 * lo, lo + hi), A(N("cut"), lo, hi), ALU.mult)
    tt(A("qfin" if last else "QS%d" % t, lo, hi), A("pC", 2 * lo, lo + hi), A(qn, lo, hi), ALU.add)
    if last:
        store("yq", A("qfin", lo, hi), lo, hi)
    else:
        send(t, s, lo, hi)
    tt(A("pC", lo + hi, 2 * hi), A("pC", lo + hi, 2 * hi), A(N("cut"), lo, hi), ALU.mult)
    tt(A("cfin" if last else "c%d" % nv, lo, hi), A("pC", lo + hi, 2 * hi), A(cn, lo, hi), ALU.add)
    if last:
        store("yc", A("cfin", lo, hi), lo, hi)
    pout = "pfin" if last else "p%d" % nv
    vcp(A(pout, lo, hi), IND(A("pool", 0, 1024), A(S("OU"), w, 2 * w)))
    if last:
        store("yp", A(pout, lo, hi), lo, hi)
        store("yz", A(nz, lo, hi), lo, hi)


def send(t, s, lo, hi):
    k = "arr%d_%d" % (t, s)

    def f(g, T, core, topo):
        dst = T.cores[(T.rank_of(core) + ST) % NR]
        rid, pid, _ = topo.addr(dst)
        g.remote_dma(T["QL%d" % t][:, lo:hi], T["QS%d" % t][:, lo:hi], T.sem[k], T.sem.sent, pid, rid, topo.mask(core, dst))
    add("G", 0.3, [f], [A("QS%d" % t, lo, hi)], [], key="sent", lat=3.5, remote=True)
    add("N", 3.5, [], [], [A("QL%d" % t, lo, hi)], key=k, after=len(OPS) - 1)


def visit(t):
    for ci in range(len(CHUNKS)):
        chunk(t, ci)
        for s, (a, b) in enumerate(SUPERS):
            if CHUNKS[ci][1] == b:
                small(t, s)
    v = t % 2
    last = t == NV - 1
    for s, (a, b) in enumerate(SUPERS):
        w = b - a
        ou = "OU_%d%d" % (s, v)
        ts(IND(A("tab", 0, 2048), A(ou, 0, w)), A("rA%d" % v, 16 * a, 16 * b), 0.5, -8388608.0, ALU.mult, ALU.add)
        e = min(5, b) - a
        if e > 0 and not last:
            ts(IND(A("tab", 2048, 2688), A(ou, 0, e)), A("rA%d" % v, 16 * a, 16 * a + 16 * e), 0.5, -8388608.0, ALU.mult, ALU.add)
    if last:
        store("yx", A("tab", 0, 2048), cast=True)
    else:
        for s, (a, b) in enumerate(SUPERS):
            hash_u(t + 1, a, b)
            for n, src in (("x", "c%d" % (1 - v)), ("y", "p%d" % (1 - v)), ("v", "QL%d" % t)):
                hash_list(n, t + 1, src, a, b)
    for s, (a, b) in enumerate(SUPERS):
        w = b - a
        vcp(IND(A("pool"), A("OU_%d%d" % (s, v), 2 * w, 3 * w)), A("cfin" if last else "c%d" % (1 - v), 16 * a, 16 * b))
    if last:
        store("yl", A("pool", 0, 1024), 0, 1024)
    else:
        nr = "nrb%d" % v
        for s, (a, b) in enumerate(SUPERS):
            vcp(A(nr, a, b), A("ka_%d" % s, 0, b - a))
        mms([(A("pZ", 384, 400), A("ones", 0, 128), A(nr), True, True)])
        out, src = A("cnt"), A("pZ", 384, 400)
        add("V", 0.06, [lambda g, T: g.vector.tensor_reduce(out["g"](T), src["g"](T), AxisListType.X, ALU.add)], [src], [out])
        vcp(A("cnti"), A("cnt"))
        ts(A("cnta"), A("cnti"), 1024, None, ALU.bitwise_and)
        ts(A("cntf"), A("cnta"), 0.25, None, ALU.mult)
        ts(A("thr%d" % (1 - v)), A("thrc"), A("cntf"), None, ALU.add)


def is_psum(name):
    return SCRATCH[name][0] == "psum"


def depend(ops):
    hist = {}
    for i, o in enumerate(ops):
        preds = set()
        if "after" in o:
            preds.add(o["after"])
        for regs, wr in ((o["R"], False), (o["W"], True)):
            for name, lo, hi in regs:
                ps = is_psum(name)
                for (j, l2, h2, w2, q2) in hist.get(name, []):
                    if j != i and ((l2 < hi and lo < h2 and (wr or w2)) or (ps and q2 != o["q"])):
                        preds.add(j)
        for regs, wr in ((o["R"], False), (o["W"], True)):
            for name, lo, hi in regs:
                L = hist.setdefault(name, [])
                if wr and not is_psum(name):
                    L[:] = [x for x in L if x[0] == i or not (lo <= x[1] and x[2] <= hi)]
                L.append((i, lo, hi, wr, o["q"]))
        o["preds"] = sorted(preds)


def schedule(ops, bias):
    n = len(ops)
    succ = [[] for _ in range(n)]
    for i, o in enumerate(ops):
        for j in o["preds"]:
            succ[j].append(i)
    lat = [o.get("lat", o["cost"]) for o in ops]
    prio = [0.0] * n
    for i in range(n - 1, -1, -1):
        prio[i] = lat[i] + max([prio[j] + (HOP if ops[j]["q"] != ops[i]["q"] else 0.02) for j in succ[i]] + [0.0])
    prio = [p + x for p, x in zip(prio, bias)]
    left = [len(o["preds"]) for o in ops]
    ready = [0.0] * n
    avail = {q: [] for q in "VSPGYN"}
    for i in range(n):
        if left[i] == 0:
            avail[ops[i]["q"]].append(i)
    free = {q: 0.0 for q in avail}
    glob = []
    while len(glob) < n:
        best = None
        for q in avail:
            if not avail[q]:
                continue
            t0 = min(max(free[q], ready[i]) for i in avail[q])
            cand = [i for i in avail[q] if max(free[q], ready[i]) <= t0 + 1e-9]
            i = max(cand, key=lambda k: prio[k])
            if best is None or t0 < best[0]:
                best = (t0, q, i)
        t0, q, i = best
        avail[q].remove(i)
        glob.append(i)
        free[q] = t0 + ops[i]["cost"] if q != "N" else 0.0
        fin = t0 + lat[i]
        for j in succ[i]:
            ready[j] = max(ready[j], fin + (HOP if ops[j]["q"] != q else 0.02))
            left[j] -= 1
            if left[j] == 0:
                avail[ops[j]["q"]].append(j)
    return glob


def evaluate(ops, glob, ga, sc, pe, hop):
    free, fin = {q: 0.0 for q in "VSPGYN"}, {}
    for i in glob:
        o = ops[i]
        q = o["q"]
        c = o["cost"] * (pe if q == "P" else 1.0) + ((ga - GA) * o["ge"] + (sc - SC) * o["se"]) * CY
        t = free[q]
        for j in o["preds"]:
            t = max(t, fin[j] + (hop if ops[j]["q"] != q else 0.02))
        if q != "N":
            free[q] = t + c
        fin[i] = t + o.get("lat", c)
    return max(fin.values())


CASES = [(1.5, 3.8, 1.0, 0.08), (1.15, 2.5, 1.0, 0.05), (1.9, 5.0, 1.0, 0.15), (1.5, 3.8, 1.3, 0.2)]


def search(ops):
    rng = np.random.default_rng(1)
    m = max(o["place"] for o in ops) + 1

    def score(glob):
        return sum(evaluate(ops, glob, *c) / (c[0] + 1.5) for c in CASES)
    best = None
    for beta in (0.0, 0.005, 0.01, 0.02):
        glob = schedule(ops, [-beta * i for i in range(len(ops))])
        s = score(glob)
        if best is None or s < best[0]:
            best = (s, beta, np.zeros(m), glob)
    for it in range(ITERS):
        d = best[2] + (rng.random(m) < 0.06) * rng.normal(0, 3.0, m)
        glob = schedule(ops, [float(d[o["place"]]) - best[1] * i for i, o in enumerate(ops)])
        s = score(glob)
        if s < best[0]:
            best = (s, best[1], d, glob)
    return best[3]


def make_plan():
    constants()
    for t in range(NV):
        START[:] = [len(OPS) - 1]
        visit(t)
    ops = OPS
    depend(ops)
    glob = search(ops)
    inc = {q: 0 for q in "VSPG"}
    dma = {}
    know = {q: {} for q in "VSPGYN"}
    for pos, i in enumerate(glob):
        o = ops[i]
        q = o["q"]
        k = know[q]
        need = {}
        if q != "N":
            for j in sorted(o["preds"], key=lambda j: -ops[j]["pos"]):
                pk, pv = ops[j]["done"]
                if max(k.get(pk, 0), need.get(pk, 0)) >= pv:
                    continue
                need[pk] = pv
                for kk, vv in ops[j]["clock"].items():
                    k[kk] = max(k.get(kk, 0), vv)
            for pk, pv in list(need.items()):
                if k.get(pk, 0) >= pv:
                    del need[pk]
                else:
                    k[pk] = pv
        o["waits"] = sorted(need.items())
        o["pos"] = pos
        if q == "N":
            o["done"] = (o["key"], 1)
            o["clock"] = {}
            continue
        o["clock"] = dict(k)
        if o["key"] is None:
            inc[q] += len(o["fns"])
            o["done"] = (q, inc[q])
        else:
            dma[o["key"]] = dma.get(o["key"], 0) + 16
            o["done"] = (o["key"], 16)
    return ops, glob, inc, dma


PLAN = make_plan()


def rank_program(g, core, T, topo):
    if T.rank_of(core) is None:
        return
    ops, glob, inc, dma = PLAN
    Q = {"V": g.vector, "S": g.scalar, "P": g.tensor, "G": g, "Y": g.sync}
    src = T.cores[(T.rank_of(core) - ST) % NR]
    dst = T.cores[(T.rank_of(core) + ST) % NR]
    nin, nout = len(topo.engines(src, core)), len(topo.engines(core, dst))
    sends = 0
    for i in glob:
        o = ops[i]
        if o["q"] == "N":
            continue
        q = Q[o["q"]]
        for k, v in o["waits"]:
            q.wait_ge(T.sem[k], nin if k[:3] == "arr" else v)
        for f in o["fns"]:
            if o.get("remote"):
                f(g, T, core, topo)
                sends += 1
            elif o["key"] is None:
                f(g, T).then_inc(T.sem[o["q"]], 1)
            else:
                f(g, T).then_inc(T.sem[o["key"]], 16)
    for k in "VSPG":
        g.sync.wait_ge(T.sem[k], inc[k])
    for k in sorted(dma):
        if k == "sent":
            g.wait_ge(T.sem.sent, nout * sends)
        elif k == "gd":
            g.wait_ge(T.sem.gd, 16)
        else:
            g.sync.wait_ge(T.sem[k], 16)
